import numpy as np
import ml_dtypes


def mxq(x, axis, fmt="e4m3"):
    dtype, down = {"e4m3": (ml_dtypes.float8_e4m3fn, 7), "e5m2": (ml_dtypes.float8_e5m2, 14)}[fmt]
    v = np.moveaxis(np.asarray(x, np.float32).astype(ml_dtypes.bfloat16).astype(np.float64), axis, -1)
    blocks = v.reshape(v.shape[:-1] + (-1, 32))
    amax = np.abs(blocks).max(-1, keepdims=True)
    byte = np.maximum(np.where(amax > 0, np.frexp(amax)[1] - 1 + 127, 0) - down, 1)
    scale = np.exp2(byte - 127.0)
    codes = (blocks / scale).astype(np.float32).astype(dtype).astype(np.float64)
    return np.moveaxis((codes * scale).reshape(v.shape), -1, axis)


WIDE = False


def mx_kscale(k):
    if not WIDE:
        return np.ones(k)
    levels = np.array([10, -10, 5, -5, 0])
    if k % 512:
        return np.exp2(np.random.permutation(np.resize(levels, k // 32))).repeat(32)
    a = np.empty((k // 512, 16))
    for p in range(k // 512):
        a[p, :8] = np.random.permutation(np.resize(levels, 8))
        for g in range(8):
            far = levels[np.abs(levels - a[p, g]) >= 10]
            a[p, g + 8] = far[np.random.randint(len(far))]
    return np.exp2(a.ravel()).repeat(32)


def f64(x):
    return np.asarray(x).astype(np.float64)


def striped(idx):
    return np.tile(idx.reshape(-1, 16).T, (8, 1)).astype(np.uint16)


def unstriped(offs):
    return offs[:16].T.reshape(-1).astype(np.int64)


K, T, E, C, N = 1024, 2048, 2, 256, 128


def by_expert(wq, xq):
    return np.concatenate([wq[e].T @ xq[:, e * C:(e + 1) * C] for e in range(E)], axis=1)


def setup_inputs():
    n = np.random.standard_normal
    s = mx_kscale(K)[:, None]
    return {
        "xT": (n((K, T)) * s).astype(np.float32),
        "w": (n((E, K, N)) / np.sqrt(K) / s[None]).astype(np.float32),
        "gate": np.tile(np.random.uniform(0.2, 1.0, E * C), (N, 1)).astype(np.float32),
        "offs": striped(np.random.permutation(T)[:E * C]),
    }


def reference(xT, w, gate, offs):
    idx = unstriped(offs)
    xq = mxq(f64(xT)[:, idx], 0, "e4m3")
    y = by_expert(mxq(f64(w), 1, "e4m3"), xq)
    out = np.zeros((N, T))
    out[:, idx] = f64(gate) * y
    return out

@@ -1,0 +1,128 @@
+from contextlib import ExitStack
+
+import concourse.mybir as mybir
+
+K, T, E, C, N = 1024, 2048, 2, 256, 128
+FLOPS = 2 * K * N * E * C
+
+F32 = mybir.dt.float32
+BF16 = mybir.dt.bfloat16
+U32 = mybir.dt.uint32
+U16 = mybir.dt.uint16
+U8 = mybir.dt.uint8
+FP8X4 = mybir.dt.float8_e4m3fn_x4
+MULT = mybir.AluOpType.mult
+
+P = 128
+PACK = 4
+K_PASS = P * PACK
+PASSES = K // K_PASS
+SLOTS = E * C
+LIST_COLS = C // 16
+
+LATE_BLOCKS = 2
+
+
+def tile_routed_moe_kernel(tc, xT, w, gate, offs, out):
+    nc = tc.nc
+    with ExitStack() as ctx:
+        keep = ctx.enter_context(tc.tile_pool(name="keep", bufs=1))
+        psum = ctx.enter_context(tc.psum_pool(name="psum", bufs=1))
+
+        offsets = keep.tile([P, SLOTS // 16], U16, name="offsets")
+        nc.sync.dma_start(offsets[:], offs)
+
+        blocks = E * PASSES
+        early = blocks - LATE_BLOCKS
+        w_blocks = w.rearrange("e (g p j) n -> (e g) p j n", p=P, j=PACK)
+        w_raw = [keep.tile([P, PACK, N], F32, name="w_raw%d" % b) for b in range(blocks - 1)]
+        w_raw.append(keep.tile([P, PACK, N], F32, name="w_raw_last", tag="turn"))
+        w_grouped = [keep.tile([P, N, PACK], BF16, name="w_grouped%d" % b, align_bytes=64) for b in range(blocks)]
+        w_codes = [keep.tile([P, N], U32, name="w_codes%d" % b, align_bytes=64) for b in range(blocks)]
+        w_scales = [keep.tile([P, N], U8, name="w_scales%d" % b, align_bytes=64) for b in range(blocks)]
+
+        for b in range(early):
+            nc.sync.dma_start(w_raw[b][:], w_blocks[b])
+        x_planes = xT.rearrange("(g p t) n -> g t p n", p=P, t=PACK)
+        planes = []
+        for g in range(PASSES):
+            for t in range(PACK):
+                plane = keep.tile([P, T], F32, name="plane%d%d" % (g, t))
+                nc.sync.dma_start(plane[:], x_planes[g, t])
+                planes.append(plane)
+        for b in range(early, blocks):
+            nc.sync.dma_start(w_raw[b][:], w_blocks[b])
+        gate_sb = keep.tile([P, SLOTS], F32, name="gate_sb")
+        nc.sync.dma_start(gate_sb[:], gate)
+
+        window = keep.tile([P, T], F32, name="window")
+        nc.vector.memset(window[:], 0.0)
+
+        def quantize_weights(b):
+            nc.scalar.copy(w_grouped[b][:], w_raw[b][:].rearrange("p j n -> p n j"))
+            nc.vector.quantize_mx(
+                out=w_codes[b][:].bitcast(FP8X4),
+                scales=w_scales[b][:],
+                in_=w_grouped[b][:].rearrange("p n j -> p (n j)"),
+            )
+
+        x_grouped = []
+        x_codes = []
+        x_scales = []
+        for g in range(PASSES):
+            x_grouped.append(keep.tile([P, SLOTS, PACK], BF16, name="x_grouped%d" % g, align_bytes=64))
+            x_codes.append(keep.tile([P, SLOTS], U32, name="x_codes%d" % g, align_bytes=64))
+            x_scales.append(keep.tile([P, SLOTS], U8, name="x_scales%d" % g, align_bytes=64))
+        accs = [psum.tile([N, C], F32, name="acc%d" % e) for e in range(E)]
+
+        def quantize_slots(g, s0, s1):
+            nc.vector.quantize_mx(
+                out=x_codes[g][:, s0:s1].bitcast(FP8X4),
+                scales=x_scales[g][:, s0:s1],
+                in_=x_grouped[g][:, s0:s1, :].rearrange("p s j -> p (s j)"),
+            )
+
+        def multiply(e, g):
+            b = e * PASSES + g
+            nc.tensor.matmul_mx(
+                out=accs[e][:],
+                lhsT=w_codes[b][:].bitcast(FP8X4),
+                lhsT_scale=w_scales[b][:],
+                rhs=x_codes[g][:, e * C:(e + 1) * C].bitcast(FP8X4),
+                rhs_scale=x_scales[g][:, e * C:(e + 1) * C],
+                start=(g == 0),
+                stop=(g == PASSES - 1),
+            )
+
+        for b in range(early):
+            quantize_weights(b)
+        for t in range(PACK):
+            nc.vector.tensor_copy(x_grouped[0][:, :, t], planes[t][:].indirect(offsets[:]))
+        quantize_slots(0, 0, SLOTS)
+        multiply(0, 0)
+        for t in range(PACK - 1):
+            nc.vector.tensor_copy(x_grouped[1][:, :, t], planes[PACK + t][:].indirect(offsets[:]))
+        for e in range(E):
+            nc.vector.tensor_copy(
+                x_grouped[1][:, e * C:(e + 1) * C, PACK - 1],
+                planes[2 * PACK - 1][:].indirect(offsets[:, e * LIST_COLS:(e + 1) * LIST_COLS]),
+            )
+            quantize_slots(1, e * C, (e + 1) * C)
+            if e == 0:
+                multiply(e, 1)
+        for b in range(early, blocks):
+            quantize_weights(b)
+        for g in range(PASSES):
+            multiply(1, g)
+
+        for e in range(E):
+            y = keep.tile([N, C], F32, name="sums%d" % e, tag=("turn" if e == 0 else "sums1"))
+            nc.scalar.copy(y[:], accs[e][:])
+            nc.vector.tensor_tensor(
+                window[:].indirect(offsets[:, e * LIST_COLS:(e + 1) * LIST_COLS]),
+                y[:],
+                gate_sb[:, e * C:(e + 1) * C],
+                MULT,
+            )
+
+        nc.sync.dma_start(out, window[:])

@@ -20,7 +20,7 @@ PASSES = K // K_PASS
 SLOTS = E * C
 LIST_COLS = C // 16
 
-LATE_BLOCKS = 2
+LATE_BLOCKS = 4
 
 
 def tile_routed_moe_kernel(tc, xT, w, gate, offs, out):
@@ -99,7 +99,13 @@ def tile_routed_moe_kernel(tc, xT, w, gate, offs, out):
         for t in range(PACK):
             nc.vector.tensor_copy(x_grouped[0][:, :, t], planes[t][:].indirect(offsets[:]))
         quantize_slots(0, 0, SLOTS)
-        multiply(0, 0)
+        ready = early
+        done = []
+        for e in range(E):
+            for g in range(PASSES - 1):
+                if e * PASSES + g < ready:
+                    multiply(e, g)
+                    done.append((e, g))
         for t in range(PACK - 1):
             nc.vector.tensor_copy(x_grouped[1][:, :, t], planes[PACK + t][:].indirect(offsets[:]))
         for e in range(E):
@@ -108,12 +114,12 @@ def tile_routed_moe_kernel(tc, xT, w, gate, offs, out):
                 planes[2 * PACK - 1][:].indirect(offsets[:, e * LIST_COLS:(e + 1) * LIST_COLS]),
             )
             quantize_slots(1, e * C, (e + 1) * C)
-            if e == 0:
-                multiply(e, 1)
-        for b in range(early, blocks):
-            quantize_weights(b)
-        for g in range(PASSES):
-            multiply(1, g)
+            for b in range(max(ready, e * PASSES), (e + 1) * PASSES):
+                quantize_weights(b)
+            ready = max(ready, (e + 1) * PASSES)
+            for g in range(PASSES):
+                if (e, g) not in done:
+                    multiply(e, g)
 
         for e in range(E):
             y = keep.tile([N, C], F32, name="sums%d" % e, tag=("turn" if e == 0 else "sums1"))

@@ -12,6 +12,7 @@ U16 = mybir.dt.uint16
 U8 = mybir.dt.uint8
 FP8X4 = mybir.dt.float8_e4m3fn_x4
 MULT = mybir.AluOpType.mult
+ADD = mybir.AluOpType.add
 
 P = 128
 PACK = 4
@@ -19,8 +20,6 @@ K_PASS = P * PACK
 PASSES = K // K_PASS
 SLOTS = E * C
 LIST_COLS = C // 16
-
-LATE_BLOCKS = 4
 
 
 def tile_routed_moe_kernel(tc, xT, w, gate, offs, out):
@@ -32,17 +31,6 @@ def tile_routed_moe_kernel(tc, xT, w, gate, offs, out):
         offsets = keep.tile([P, SLOTS // 16], U16, name="offsets")
         nc.sync.dma_start(offsets[:], offs)
 
-        blocks = E * PASSES
-        early = blocks - LATE_BLOCKS
-        w_blocks = w.rearrange("e (g p j) n -> (e g) p j n", p=P, j=PACK)
-        w_raw = [keep.tile([P, PACK, N], F32, name="w_raw%d" % b) for b in range(blocks - 1)]
-        w_raw.append(keep.tile([P, PACK, N], F32, name="w_raw_last", tag="turn"))
-        w_grouped = [keep.tile([P, N, PACK], BF16, name="w_grouped%d" % b, align_bytes=64) for b in range(blocks)]
-        w_codes = [keep.tile([P, N], U32, name="w_codes%d" % b, align_bytes=64) for b in range(blocks)]
-        w_scales = [keep.tile([P, N], U8, name="w_scales%d" % b, align_bytes=64) for b in range(blocks)]
-
-        for b in range(early):
-            nc.sync.dma_start(w_raw[b][:], w_blocks[b])
         x_planes = xT.rearrange("(g p t) n -> g t p n", p=P, t=PACK)
         planes = []
         for g in range(PASSES):
@@ -50,20 +38,43 @@ def tile_routed_moe_kernel(tc, xT, w, gate, offs, out):
                 plane = keep.tile([P, T], F32, name="plane%d%d" % (g, t))
                 nc.sync.dma_start(plane[:], x_planes[g, t])
                 planes.append(plane)
-        for b in range(early, blocks):
-            nc.sync.dma_start(w_raw[b][:], w_blocks[b])
+
+        w_blocks = w.rearrange("e (g p j) n -> e g p j n", p=P, j=PACK)
         gate_sb = keep.tile([P, SLOTS], F32, name="gate_sb")
+        w_raw = {}
+        for e in range(E):
+            for g in range(PASSES):
+                last = e == E - 1 and g == PASSES - 1
+                w_raw[e, g] = keep.tile([P, PACK, N], F32, name="w_raw%d%d" % (e, g), tag=("w_rawl" if last else "w_raw%d%d" % (e, g)))
+                nc.sync.dma_start(w_raw[e, g][:], w_blocks[e, g])
         nc.sync.dma_start(gate_sb[:], gate)
 
         window = keep.tile([P, T], F32, name="window")
         nc.vector.memset(window[:], 0.0)
 
-        def quantize_weights(b):
-            nc.scalar.copy(w_grouped[b][:], w_raw[b][:].rearrange("p j n -> p n j"))
+        w_grouped = {}
+        w_codes = {}
+        w_scales = {}
+        for e in range(E):
+            for g in range(PASSES):
+                w_grouped[e, g] = keep.tile([P, N, PACK], BF16, name="w_grouped%d%d" % (e, g), align_bytes=64)
+                w_codes[e, g] = keep.tile([P, N], U32, name="w_codes%d%d" % (e, g), align_bytes=64)
+                w_scales[e, g] = keep.tile([P, N], U8, name="w_scales%d%d" % (e, g), align_bytes=64)
+
+        def interleave_weights(e, g):
+            b = e * PASSES + g
+            if b in []:
+                nc.gpsimd.tensor_scalar(out=w_grouped[e, g][:], in0=w_raw[e, g][:].rearrange("p j n -> p n j"), scalar1=1.0, scalar2=0.0, op0=MULT, op1=ADD)
+            elif b in []:
+                nc.vector.tensor_copy(w_grouped[e, g][:], w_raw[e, g][:].rearrange("p j n -> p n j"))
+            else:
+                nc.scalar.copy(w_grouped[e, g][:], w_raw[e, g][:].rearrange("p j n -> p n j"))
+
+        def quantize_weights(e, g):
             nc.vector.quantize_mx(
-                out=w_codes[b][:].bitcast(FP8X4),
-                scales=w_scales[b][:],
-                in_=w_grouped[b][:].rearrange("p n j -> p (n j)"),
+                out=w_codes[e, g][:].bitcast(FP8X4),
+                scales=w_scales[e, g][:],
+                in_=w_grouped[e, g][:].rearrange("p n j -> p (n j)"),
             )
 
         x_grouped = []
@@ -83,29 +94,19 @@ def tile_routed_moe_kernel(tc, xT, w, gate, offs, out):
             )
 
         def multiply(e, g):
-            b = e * PASSES + g
             nc.tensor.matmul_mx(
                 out=accs[e][:],
-                lhsT=w_codes[b][:].bitcast(FP8X4),
-                lhsT_scale=w_scales[b][:],
+                lhsT=w_codes[e, g][:].bitcast(FP8X4),
+                lhsT_scale=w_scales[e, g][:],
                 rhs=x_codes[g][:, e * C:(e + 1) * C].bitcast(FP8X4),
                 rhs_scale=x_scales[g][:, e * C:(e + 1) * C],
                 start=(g == 0),
                 stop=(g == PASSES - 1),
             )
 
-        for b in range(early):
-            quantize_weights(b)
         for t in range(PACK):
             nc.vector.tensor_copy(x_grouped[0][:, :, t], planes[t][:].indirect(offsets[:]))
         quantize_slots(0, 0, SLOTS)
-        ready = early
-        done = []
-        for e in range(E):
-            for g in range(PASSES - 1):
-                if e * PASSES + g < ready:
-                    multiply(e, g)
-                    done.append((e, g))
         for t in range(PACK - 1):
             nc.vector.tensor_copy(x_grouped[1][:, :, t], planes[PACK + t][:].indirect(offsets[:]))
         for e in range(E):
@@ -114,16 +115,18 @@ def tile_routed_moe_kernel(tc, xT, w, gate, offs, out):
                 planes[2 * PACK - 1][:].indirect(offsets[:, e * LIST_COLS:(e + 1) * LIST_COLS]),
             )
             quantize_slots(1, e * C, (e + 1) * C)
-            for b in range(max(ready, e * PASSES), (e + 1) * PASSES):
-                quantize_weights(b)
-            ready = max(ready, (e + 1) * PASSES)
             for g in range(PASSES):
-                if (e, g) not in done:
-                    multiply(e, g)
+                interleave_weights(e, g)
+                quantize_weights(e, g)
+            for g in range(PASSES):
+                multiply(e, g)
 
         for e in range(E):
-            y = keep.tile([N, C], F32, name="sums%d" % e, tag=("turn" if e == 0 else "sums1"))
-            nc.scalar.copy(y[:], accs[e][:])
+            y = keep.tile([N, C], F32, name="sums%d" % e, tag=("sums0" if e == 0 else "sums1"))
+            if e == 0:
+                nc.vector.tensor_copy(y[:], accs[e][:])
+            else:
+                nc.scalar.copy(y[:], accs[e][:])
             nc.vector.tensor_tensor(
                 window[:].indirect(offsets[:, e * LIST_COLS:(e + 1) * LIST_COLS]),
                 y[:],

@@ -122,16 +122,13 @@ def tile_routed_moe_kernel(tc, xT, w, gate, offs, out):
                 multiply(e, g)
 
         for e in range(E):
-            y = keep.tile([N, C], F32, name="sums%d" % e, tag=("sums0" if e == 0 else "sums1"))
+            y = keep.tile([N, C], F32, name="sums%d" % e)
+            slots = offsets[:, e * LIST_COLS:(e + 1) * LIST_COLS]
             if e == 0:
-                nc.vector.tensor_copy(y[:], accs[e][:])
+                nc.vector.tensor_tensor(y[:], accs[e][:], gate_sb[:, e * C:(e + 1) * C], MULT)
+                nc.vector.tensor_copy(window[:].indirect(slots), y[:])
             else:
                 nc.scalar.copy(y[:], accs[e][:])
-            nc.vector.tensor_tensor(
-                window[:].indirect(offsets[:, e * LIST_COLS:(e + 1) * LIST_COLS]),
-                y[:],
-                gate_sb[:, e * C:(e + 1) * C],
-                MULT,
-            )
+                nc.vector.tensor_tensor(window[:].indirect(slots), y[:], gate_sb[:, e * C:(e + 1) * C], MULT)
 
         nc.sync.dma_start(out, window[:])

@@ -104,8 +104,10 @@ def tile_routed_moe_kernel(tc, xT, w, gate, offs, out):
                 stop=(g == PASSES - 1),
             )
 
+        picked = keep.tile([P, PACK, SLOTS], F32, name="picked")
         for t in range(PACK):
-            nc.vector.tensor_copy(x_grouped[0][:, :, t], planes[t][:].indirect(offsets[:]))
+            nc.vector.tensor_copy(picked[:, t, :], planes[t][:].indirect(offsets[:]))
+        nc.scalar.copy(x_grouped[0][:], picked[:].rearrange("p t s -> p s t"))
         quantize_slots(0, 0, SLOTS)
         for t in range(PACK - 1):
             nc.vector.tensor_copy(x_grouped[1][:, :, t], planes[PACK + t][:].indirect(offsets[:]))

from contextlib import ExitStack

import concourse.mybir as mybir

K, T, E, C, N = 1024, 2048, 2, 256, 128
FLOPS = 2 * K * N * E * C

F32 = mybir.dt.float32
BF16 = mybir.dt.bfloat16
U32 = mybir.dt.uint32
U16 = mybir.dt.uint16
U8 = mybir.dt.uint8
FP8X4 = mybir.dt.float8_e4m3fn_x4
MULT = mybir.AluOpType.mult
ADD = mybir.AluOpType.add

P = 128
PACK = 4
K_PASS = P * PACK
PASSES = K // K_PASS
SLOTS = E * C
LIST_COLS = C // 16


def tile_routed_moe_kernel(tc, xT, w, gate, offs, out):
    nc = tc.nc
    with ExitStack() as ctx:
        keep = ctx.enter_context(tc.tile_pool(name="keep", bufs=1))
        psum = ctx.enter_context(tc.psum_pool(name="psum", bufs=1))

        offsets = keep.tile([P, SLOTS // 16], U16, name="offsets")
        nc.sync.dma_start(offsets[:], offs)

        x_planes = xT.rearrange("(g p t) n -> g t p n", p=P, t=PACK)
        planes = []
        for g in range(PASSES):
            for t in range(PACK):
                plane = keep.tile([P, T], F32, name="plane%d%d" % (g, t))
                nc.sync.dma_start(plane[:], x_planes[g, t])
                planes.append(plane)

        w_blocks = w.rearrange("e (g p j) n -> e g p j n", p=P, j=PACK)
        gate_sb = keep.tile([P, SLOTS], F32, name="gate_sb")
        w_raw = {}
        for e in range(E):
            for g in range(PASSES):
                last = e == E - 1 and g == PASSES - 1
                w_raw[e, g] = keep.tile([P, PACK, N], F32, name="w_raw%d%d" % (e, g), tag=("w_rawl" if last else "w_raw%d%d" % (e, g)))
                nc.sync.dma_start(w_raw[e, g][:], w_blocks[e, g])
        nc.sync.dma_start(gate_sb[:], gate)

        window = keep.tile([P, T], F32, name="window")
        nc.vector.memset(window[:], 0.0)

        w_grouped = {}
        w_codes = {}
        w_scales = {}
        for e in range(E):
            for g in range(PASSES):
                w_grouped[e, g] = keep.tile([P, N, PACK], BF16, name="w_grouped%d%d" % (e, g), align_bytes=64)
                w_codes[e, g] = keep.tile([P, N], U32, name="w_codes%d%d" % (e, g), align_bytes=64)
                w_scales[e, g] = keep.tile([P, N], U8, name="w_scales%d%d" % (e, g), align_bytes=64)

        def interleave_weights(e, g):
            b = e * PASSES + g
            if b in []:
                nc.gpsimd.tensor_scalar(out=w_grouped[e, g][:], in0=w_raw[e, g][:].rearrange("p j n -> p n j"), scalar1=1.0, scalar2=0.0, op0=MULT, op1=ADD)
            elif b in []:
                nc.vector.tensor_copy(w_grouped[e, g][:], w_raw[e, g][:].rearrange("p j n -> p n j"))
            else:
                nc.scalar.copy(w_grouped[e, g][:], w_raw[e, g][:].rearrange("p j n -> p n j"))

        def quantize_weights(e, g):
            nc.vector.quantize_mx(
                out=w_codes[e, g][:].bitcast(FP8X4),
                scales=w_scales[e, g][:],
                in_=w_grouped[e, g][:].rearrange("p n j -> p (n j)"),
            )

        x_grouped = []
        x_codes = []
        x_scales = []
        for g in range(PASSES):
            x_grouped.append(keep.tile([P, SLOTS, PACK], BF16, name="x_grouped%d" % g, align_bytes=64))
            x_codes.append(keep.tile([P, SLOTS], U32, name="x_codes%d" % g, align_bytes=64))
            x_scales.append(keep.tile([P, SLOTS], U8, name="x_scales%d" % g, align_bytes=64))
        accs = [psum.tile([N, C], F32, name="acc%d" % e) for e in range(E)]

        def quantize_slots(g, s0, s1):
            nc.vector.quantize_mx(
                out=x_codes[g][:, s0:s1].bitcast(FP8X4),
                scales=x_scales[g][:, s0:s1],
                in_=x_grouped[g][:, s0:s1, :].rearrange("p s j -> p (s j)"),
            )

        def multiply(e, g):
            nc.tensor.matmul_mx(
                out=accs[e][:],
                lhsT=w_codes[e, g][:].bitcast(FP8X4),
                lhsT_scale=w_scales[e, g][:],
                rhs=x_codes[g][:, e * C:(e + 1) * C].bitcast(FP8X4),
                rhs_scale=x_scales[g][:, e * C:(e + 1) * C],
                start=(g == 0),
                stop=(g == PASSES - 1),
            )

        picked = keep.tile([P, PACK, SLOTS], F32, name="picked")
        for t in range(PACK):
            nc.vector.tensor_copy(picked[:, t, :], planes[t][:].indirect(offsets[:]))
        nc.scalar.copy(x_grouped[0][:], picked[:].rearrange("p t s -> p s t"))
        quantize_slots(0, 0, SLOTS)
        for t in range(PACK - 1):
            nc.vector.tensor_copy(x_grouped[1][:, :, t], planes[PACK + t][:].indirect(offsets[:]))
        for e in range(E):
            nc.vector.tensor_copy(
                x_grouped[1][:, e * C:(e + 1) * C, PACK - 1],
                planes[2 * PACK - 1][:].indirect(offsets[:, e * LIST_COLS:(e + 1) * LIST_COLS]),
            )
            quantize_slots(1, e * C, (e + 1) * C)
            for g in range(PASSES):
                interleave_weights(e, g)
                quantize_weights(e, g)
            for g in range(PASSES):
                multiply(e, g)

        for e in range(E):
            y = keep.tile([N, C], F32, name="sums%d" % e)
            slots = offsets[:, e * LIST_COLS:(e + 1) * LIST_COLS]
            if e == 0:
                nc.vector.tensor_tensor(y[:], accs[e][:], gate_sb[:, e * C:(e + 1) * C], MULT)
                nc.vector.tensor_copy(window[:].indirect(slots), y[:])
            else:
                nc.scalar.copy(y[:], accs[e][:])
                nc.vector.tensor_tensor(window[:].indirect(slots), y[:], gate_sb[:, e * C:(e + 1) * C], MULT)

        nc.sync.dma_start(out, window[:])
